import numpy as np, ml_dtypes
CORES = [17,81,89,18,82,90]
N = 6
import mx_ref
NC, G, D = 512, 4, 2
C = np.float32(0.037)
BF = ml_dtypes.bfloat16
def cut(t, i, w=512):
    return t[:, w * i:w * i + w]
def tile(rs):
    return np.stack(rs, axis=2).reshape(128, -1).astype(BF)
def layer(w, X):
    out = []
    for i in range(G):
        for t in range(len(X)):
            p = mx_ref.matmul(mx_ref.quantize(cut(w, len(X) * i + t)), X[t])
            z = p if t == 0 else z + p
        out.append(z)
    return out
def act(Z):
    return [np.maximum(z, 0) * C for z in Z]
def setup_inputs(rng):
    def f(*shape):
        return mx_ref.flush((rng.standard_normal(shape, dtype=np.float32) * np.exp2(rng.integers(-2, 3, shape[:-1] + (1,)))).astype(BF))
    return {"x": f(N, 128, 4 * NC), "w1": f(N, 128, G * 512), "wt": f(N, 128, 3 * 512)}
def setup_inputs_blocks(rng):
    d = setup_inputs(rng)
    for k in ("x", "wt", "w1"): d[k] = mx_ref.spread(d[k], rng, 2)
    return d
def setup_inputs_wide(rng):
    d = setup_inputs(rng)
    for k in ("wt",): d[k] = mx_ref.flush((d[k].astype(np.float32) * np.exp2(rng.integers(-6, 7, (N, 1, 1))).astype(np.float32)).astype(BF))
    return d
def setup_inputs_zeros(rng):
    d = setup_inputs(rng); v = d["x"].reshape(N, 128, -1, 4).copy()
    v[np.broadcast_to((rng.random((N, 1, v.shape[2], 1)) < 0.33), v.shape)] = 0
    d["x"] = v.reshape(d["x"].shape)
    return d
def reference(x, w1, wt):
    h = [tile(act(layer(w1[j], [mx_ref.quantize(x[j])]))) for j in range(N)]
    y = np.zeros((N, 128, NC), np.float32)
    for r in range(N):
        e = np.concatenate([h[(r - 1) % N][:, 4 * (NC - D):], h[r], h[(r + 1) % N][:, :4 * D]], axis=1)
        for t in range(3):
            p = mx_ref.matmul(mx_ref.quantize(cut(wt[r], t)), mx_ref.quantize(e[:, 4 * D * t:4 * D * t + 4 * NC]))
            y[r] = p if t == 0 else y[r] + p
    return {"y": y}

from concourse.bass import DstId, RemoteDMATransfer
from concourse.mybir import dt, AluOpType, ActivationFunctionType

NC = 512
D = 2
C = 0.037
EW = 128
H = EW // 2
RW = NC - EW
O = 16
PW = 8

SCRATCH = {
    "xt": ("sbuf", [128, 4 * NC], "bfloat16"),
    "w1t": ("sbuf", [128, 4 * NC], "bfloat16"),
    "wtt": ("sbuf", [128, 3 * 512], "bfloat16"),
    "xq": ("sbuf", [128, NC], "float8_e4m3fn_x4"),
    "xs": ("sbuf", [128, NC], "uint8"),
    "w1q": ("sbuf", [128, 512], "float8_e4m3fn_x4"),
    "w1s": ("sbuf", [128, 512], "uint8"),
    "wtq": ("sbuf", [128, 384], "float8_e4m3fn_x4"),
    "wts": ("sbuf", [128, 384], "uint8"),
    "ht": ("sbuf", [128, 4 * (NC + H)], "bfloat16"),
    "qe": ("sbuf", [128, EW], "float8_e4m3fn_x4"),
    "se": ("sbuf", [128, EW], "uint8"),
    "e": ("sbuf", [128, NC + 2 * O], "float8_e4m3fn_x4"),
    "es": ("sbuf", [128, NC + 2 * O], "uint8"),
    "rc": ("sbuf", [128, 2 * D], "float8_e4m3fn_x4"),
    "rs": ("sbuf", [128, 2 * PW], "uint8"),
    "yt": ("sbuf", [128, NC], "float32"),
    "pe": ("psum", [128, 4 * 512], "float32"),
    "pr": ("psum", [128, 4 * 512], "float32"),
}
SEMAPHORES = (["lxe", "lw0", "lw1", "lxr", "lwt", "qxe", "qxr", "qwt", "qh", "qE", "hcopy", "aes", "aev", "ars", "arv",
               "halo_last", "halo_first", "relayed", "sent", "mA", "mB", "mM", "cA", "cB", "cM", "stA", "stB", "stM"]
              + ["qw%d" % b for b in range(4)] + ["me%d" % b for b in range(4)] + ["mr%d" % b for b in range(4)])

LEGS = ("last", "first")


def _bits(mask):
    return [1 << i for i in range(mask.bit_length()) if mask >> i & 1]


def _legs(core, T, topo):
    n = len(T.cores)
    r = T.rank_of(core)
    out = {}
    for leg, dst in (("last", T.cores[(r + 1) % n]), ("first", T.cores[(r - 1) % n])):
        via = dst
        if not topo.may_write(core, dst):
            via = [c for c in T.cores if c != core and topo.chip(c) == topo.chip(core) and topo.may_write(c, dst)][0]
        out[leg] = (dst, via)
    return out


def _send(g, T, topo, core, items, engines):
    k = len(engines) // len(items)
    tr = []
    for i, (dst, sem, src, out) in enumerate(items):
        rid, pid, _ = topo.addr(dst)
        tr.append(RemoteDMATransfer(dst_ids=[DstId(rid=rid, pnc=pid)], dma_engine_mask=sum(engines[k * i:k * i + k]),
                                    remote_sem=sem, src=src, dst=out))
    g.remote_dma_fused(tr, local_sem=T.sem.sent)
    return k * len(items)


def _columns(leg):
    if leg == "last":
        return ((H - D, H), (H - PW, H)), ((0, D), (0, PW)), ((O - D, O), (O - PW, O))
    return ((H, H + D), (H, H + PW)), ((D, 2 * D), (PW, 2 * PW)), ((O + NC, O + NC + D), (O + NC, O + NC + PW))


def _codes(t, ab):
    return t[:, ab[0]:ab[1]].bitcast(dt.uint8)


def _plane(t, ab):
    return t[:, ab[0]:ab[1]]


CALL_ENGINES = 8


def _halo(g, core, T, topo):
    legs = _legs(core, T, topo)
    sent = 0
    direct = [leg for leg in LEGS if legs[leg][0] == legs[leg][1]]
    handed = [leg for leg in LEGS if leg not in direct]
    off = 0
    for leg in direct:
        off |= topo.mask(core, legs[leg][0])
    g.wait_ge(T.sem.qh, 1)
    if handed:
        via = legs[handed[0]][1]
        assert all(legs[leg][1] == via for leg in handed)
        src = [_columns(leg)[0] for leg in handed]
        dst = [_columns(leg)[1] for leg in handed]
        (c0, s0), (c1, s1) = src[0], src[-1]
        (rc0, rs0), (rc1, rs1) = dst[0], dst[-1]
        engines = _bits(topo.mask(core, via) & ~off)[:CALL_ENGINES]
        sent += _send(g, T, topo, core, [
            (via, T.sem.relayed, _codes(T.qe, (c0[0], c1[1])), _codes(T.rc, (rc0[0], rc1[1]))),
            (via, T.sem.relayed, _plane(T.se, (s0[0], s1[1])), _plane(T.rs, (rs0[0], rs1[1])))], engines)
    if direct:
        items = []
        for leg in direct:
            to = legs[leg][0]
            src, _, dst = _columns(leg)
            sem = T.sem["halo_" + leg]
            items.append((to, sem, _codes(T.qe, src[0]), _codes(T.e, dst[0])))
            items.append((to, sem, _plane(T.se, src[1]), _plane(T.es, dst[1])))
        sent += _send(g, T, topo, core, items, _bits(off)[:CALL_ENGINES])
    for s in T.cores:
        if s == core:
            continue
        theirs = _legs(s, T, topo)
        mine = [leg for leg in LEGS if theirs[leg][1] == core and theirs[leg][0] != core]
        if not mine:
            continue
        g.wait_ge(T.sem.relayed, CALL_ENGINES)
        items = []
        m = 0xFFFFFFFF
        for leg in mine:
            to = theirs[leg][0]
            m &= topo.mask(core, to)
            _, src, dst = _columns(leg)
            sem = T.sem["halo_" + leg]
            items.append((to, sem, _codes(T.rc, src[0]), _codes(T.e, dst[0])))
            items.append((to, sem, _plane(T.rs, src[1]), _plane(T.es, dst[1])))
        sent += _send(g, T, topo, core, items, _bits(m)[:CALL_ENGINES])
    g.wait_ge(T.sem.sent, sent)


def _arrivals(core, T, topo):
    n = len(T.cores)
    r = T.rank_of(core)
    out = {}
    for leg, s in (("last", T.cores[(r - 1) % n]), ("first", T.cores[(r + 1) % n])):
        legs = _legs(s, T, topo)
        via = legs[leg][1]
        if via == core:
            calls = [l for l in LEGS if legs[l][0] == legs[l][1]]
        else:
            calls = [l for l in LEGS if legs[l][1] == via]
        out[leg] = (CALL_ENGINES // len(calls), via != core)
    return out


def rank_program(g, core, T, topo):
    if T.rank_of(core) is None:
        return
    S = T.sem
    v, s, t, y = g.vector, g.scalar, g.tensor, g.sync
    relu = ActivationFunctionType.Relu

    y.dma_start(T.xt[:, 0:4 * H], T.x[:, 4 * (NC - H):4 * NC]).then_inc(S.lxe, 16)
    s.dma_start(T.xt[:, 4 * H:8 * H], T.x[:, 0:4 * H]).then_inc(S.lxe, 16)
    y.dma_start(T.w1t[:, 0:1024], T.w1[:, 0:1024]).then_inc(S.lw0, 16)
    s.dma_start(T.w1t[:, 1024:2048], T.w1[:, 1024:2048]).then_inc(S.lw1, 16)
    y.dma_start(T.xt[:, 4 * EW:4 * NC], T.x[:, 4 * H:4 * (NC - H)]).then_inc(S.lxr, 16)
    s.dma_start(T.wtt[:], T.wt[:]).then_inc(S.lwt, 16)

    def quant(q, sc, a, b, src, sem):
        v.quantize_mx(q[:, a:b], sc[:, a:b], src).then_inc(sem, 1)

    v.wait_ge(S.lxe, 32)
    quant(T.xq, T.xs, 0, EW, T.xt[:, 0:4 * EW], S.qxe)
    t.wait_ge(S.qxe, 1)
    for b in range(4):
        if b % 2 == 0:
            v.wait_ge(S["lw%d" % (b // 2)], 16)
        quant(T.w1q, T.w1s, 128 * b, 128 * b + 128, T.w1t[:, 512 * b:512 * b + 512], S["qw%d" % b])
        t.wait_ge(S["qw%d" % b], 1)
        t.matmul_mx(T.pe[:, 512 * b:512 * b + EW], T.w1q[:, 128 * b:128 * b + 128], T.w1s[:, 128 * b:128 * b + 128],
                    T.xq[:, 0:EW], T.xs[:, 0:EW], True, True).then_inc(S["me%d" % b], 1)
    for b in range(3):
        s.wait_ge(S["me%d" % b], 1)
        s.activation(T.ht[:, b:4 * EW:4], T.pe[:, 512 * b:512 * b + EW], relu, scale=C).then_inc(S.aes, 1)
    v.wait_ge(S.me3, 1)
    v.tensor_scalar(T.ht[:, 3:4 * EW:4], T.pe[:, 1536:1536 + EW], C, 0.0, AluOpType.mult, AluOpType.max).then_inc(S.aev, 1)
    v.wait_ge(S.aes, 3)
    v.wait_ge(S.aev, 1)
    quant(T.qe, T.se, 0, EW, T.ht[:, 0:4 * EW], S.qh)

    _halo(g, core, T, topo)

    v.tensor_copy(T.ht[:, 4 * NC:4 * (NC + H)], T.ht[:, 0:4 * H]).then_inc(S.hcopy, 1)
    v.wait_ge(S.lxr, 16)
    quant(T.xq, T.xs, EW, NC, T.xt[:, 4 * EW:4 * NC], S.qxr)
    t.wait_ge(S.qxr, 1)
    for b in range(4):
        t.matmul_mx(T.pr[:, 512 * b:512 * b + RW], T.w1q[:, 128 * b:128 * b + 128], T.w1s[:, 128 * b:128 * b + 128],
                    T.xq[:, EW:NC], T.xs[:, EW:NC], True, True).then_inc(S["mr%d" % b], 1)
    for b in range(3):
        s.wait_ge(S["mr%d" % b], 1)
        s.activation(T.ht[:, 4 * EW + b:4 * NC:4], T.pr[:, 512 * b:512 * b + RW], relu, scale=C).then_inc(S.ars, 1)
    v.wait_ge(S.lwt, 16)
    quant(T.wtq, T.wts, 0, 384, T.wtt[:], S.qwt)
    v.wait_ge(S.mr3, 1)
    v.tensor_scalar(T.ht[:, 4 * EW + 3:4 * NC:4], T.pr[:, 1536:1536 + RW], C, 0.0, AluOpType.mult, AluOpType.max).then_inc(S.arv, 1)
    v.wait_ge(S.hcopy, 1)
    v.wait_ge(S.ars, 3)
    v.wait_ge(S.arv, 1)
    quant(T.e, T.es, O, O + NC, T.ht[:, 4 * H:4 * (H + NC)], S.qE)

    A, M, B = (0, 0, 128), (1024, 128, 384), (512, 384, 512)

    def tap(piece, k, start, stop):
        bank, a, b = piece
        lo = O + D * (k - 1) + a
        return t.matmul_mx(T.pe[:, bank:bank + b - a], T.wtq[:, 128 * k:128 * k + 128], T.wts[:, 128 * k:128 * k + 128],
                           T.e[:, lo:lo + b - a], T.es[:, lo:lo + b - a], start, stop)

    t.wait_ge(S.qwt, 1)
    t.wait_ge(S.qE, 1)
    tap(M, 0, True, False)
    tap(M, 1, False, False)
    tap(M, 2, False, True).then_inc(S.mM, 1)
    tap(A, 1, True, False)
    tap(A, 2, False, False)
    tap(B, 0, True, False)
    tap(B, 1, False, False)
    arrivals = _arrivals(core, T, topo)
    for leg in sorted(LEGS, key=lambda l: arrivals[l][1]):
        t.wait_ge(S["halo_" + leg], arrivals[leg][0])
        if leg == "last":
            tap(A, 0, False, True).then_inc(S.mA, 1)
        else:
            tap(B, 2, False, True).then_inc(S.mB, 1)

    v.wait_ge(S.mM, 1)
    v.tensor_copy(T.yt[:, 128:384], T.pe[:, 1024:1280]).then_inc(S.cM, 1)
    y.wait_ge(S.cM, 1)
    y.dma_start(T.y[:, 128:384], T.yt[:, 128:384]).then_inc(S.stM, 16)
    v.wait_ge(S.mA, 1)
    v.tensor_copy(T.yt[:, 0:128], T.pe[:, 0:128]).then_inc(S.cA, 1)
    y.wait_ge(S.cA, 1)
    y.dma_start(T.y[:, 0:128], T.yt[:, 0:128]).then_inc(S.stA, 16)
    s.wait_ge(S.mB, 1)
    s.activation(T.yt[:, 384:512], T.pe[:, 512:640], ActivationFunctionType.Copy).then_inc(S.cB, 1)
    s.wait_ge(S.cB, 1)
    s.dma_start(T.y[:, 384:512], T.yt[:, 384:512]).then_inc(S.stB, 16)
    y.wait_ge(S.stM, 16)
    y.wait_ge(S.stA, 16)
    s.wait_ge(S.stB, 16)
